import numpy as np
import ml_dtypes


def mxq(x, axis, fmt="e4m3"):
    dtype, down = {"e4m3": (ml_dtypes.float8_e4m3fn, 7), "e5m2": (ml_dtypes.float8_e5m2, 14)}[fmt]
    v = np.moveaxis(np.asarray(x, np.float32).astype(ml_dtypes.bfloat16).astype(np.float64), axis, -1)
    blocks = v.reshape(v.shape[:-1] + (-1, 32))
    amax = np.abs(blocks).max(-1, keepdims=True)
    byte = np.maximum(np.where(amax > 0, np.frexp(amax)[1] - 1 + 127, 0) - down, 1)
    scale = np.exp2(byte - 127.0)
    codes = (blocks / scale).astype(np.float32).astype(dtype).astype(np.float64)
    return np.moveaxis((codes * scale).reshape(v.shape), -1, axis)


WIDE = False


def mx_kscale(k):
    if not WIDE:
        return np.ones(k)
    levels = np.array([10, -10, 5, -5, 0])
    if k % 512:
        return np.exp2(np.random.permutation(np.resize(levels, k // 32))).repeat(32)
    a = np.empty((k // 512, 16))
    for p in range(k // 512):
        a[p, :8] = np.random.permutation(np.resize(levels, 8))
        for g in range(8):
            far = levels[np.abs(levels - a[p, g]) >= 10]
            a[p, g + 8] = far[np.random.randint(len(far))]
    return np.exp2(a.ravel()).repeat(32)


def f64(x):
    return np.asarray(x).astype(np.float64)


def striped(idx):
    return np.tile(np.asarray(idx).reshape(-1, 16).T, (8, 1)).astype(np.uint16)


def unstriped(offs):
    return offs[:16].T.reshape(-1).astype(np.int64)


B, N, C, D, NQ = 1, 256, 512, 512, 512


def eight(codes):
    return np.concatenate([codes[h].reshape(-1, 16).T for h in range(8)]).astype(np.uint16)


def uneight(offs):
    return np.stack([offs[16 * h:16 * h + 16].T.reshape(-1) for h in range(8)]).astype(np.int64)


def setup_inputs():
    n = np.random.standard_normal
    s = mx_kscale(D)[:, None]
    grid = lambda x: np.round(x * 32) / 32
    return {
        "qT": (n((B, D, NQ)) * s / np.sqrt(D)).astype(np.float32),
        "cb": (grid(n((D, C))) / s).astype(np.float32),
        "norm": np.tile(np.random.randint(32, 129, N) / 64.0, (128, 1)).astype(np.float32),
        "offs": eight(np.random.randint(0, C, (8, N))),
    }


def reference(qT, cb, norm, offs):
    k = []
    for part, offs_ in enumerate((offs,)):
        codes = uneight(offs_)
        k += [f64(cb)[512 * part + 64 * h:512 * part + 64 * h + 64][:, codes[h]] for h in range(8)]
    k = np.concatenate(k) * f64(norm)[:1]
    a = mxq(f64(qT), 1, "e4m3").transpose(0, 2, 1) @ mxq(k, 0, "e4m3")
    return a

@@ -1,0 +1,112 @@
+from contextlib import ExitStack
+
+import concourse.mybir as mybir
+
+D, C, N, Q = 512, 512, 256, 512
+
+F32 = mybir.dt.float32
+BF16 = mybir.dt.bfloat16
+U16 = mybir.dt.uint16
+U32 = mybir.dt.uint32
+U8 = mybir.dt.uint8
+FP8X4 = mybir.dt.float8_e4m3fn_x4
+MULT = mybir.AluOpType.mult
+
+P = 128
+T = 4
+HALF = 128
+
+FLOPS = 2 * D * Q * N
+
+
+def interleaved(nc_copy, dst, src):
+    nc_copy(
+        out=dst.rearrange("p (c i) t -> p c t i", i=4),
+        in_=src.rearrange("p t (c i) -> p c t i", i=4),
+    )
+
+
+def tile_attend_pq_lin_kernel(tc, qT, cb, norm, offs, out):
+    nc = tc.nc
+    with ExitStack() as ctx:
+        keep = ctx.enter_context(tc.tile_pool(name="keep", bufs=1))
+        psum = ctx.enter_context(tc.psum_pool(name="psum", bufs=1))
+
+        offsets = keep.tile([P, N // 16], U16, name="offsets")
+        nc.sync.dma_start(offsets[:], offs)
+        norm_sb = keep.tile([P, N], F32, name="norm_sb")
+        nc.sync.dma_start(norm_sb[:], norm)
+
+        cb_rows = cb.rearrange("(p t) c -> p t c", t=T)
+        books = []
+        for t in range(T):
+            book = keep.tile([P, C], F32, name=f"book{t}")
+            nc.sync.dma_start(book[:], cb_rows[:, t, :])
+            books.append(book)
+
+        q_rows = qT[0].rearrange("(p t) q -> p t q", t=T)
+        raws = []
+        for h in range(2):
+            raw = keep.tile([P, T, 256], F32, name=f"raw{h}")
+            nc.sync.dma_start(raw[:], q_rows[:, :, 256 * h : 256 * h + 256])
+            raws.append(raw)
+
+        dummy = keep.tile([P, 1], F32, name="dummy")
+        dummy2 = keep.tile([P, 1], F32, name="dummy2")
+        nc.gpsimd.memset(dummy[:], 0.0)
+        nc.scalar.copy(out=dummy2[:], in_=dummy[:])
+
+        ks = [keep.tile([P, T, HALF], F32, name=f"ks{h}") for h in range(2)]
+        kb = [keep.tile([P, HALF, T], BF16, name=f"kb{h}", align_bytes=64) for h in range(2)]
+        k_codes = keep.tile([P, N], U32, name="k_codes", align_bytes=64)
+        k_scales = keep.tile([P, N], U8, name="k_scales", align_bytes=64)
+        qb = [keep.tile([P, P, T], BF16, name=f"qb{m}", align_bytes=64) for m in range(4)]
+        q_codes = [keep.tile([P, P], U32, name=f"q_codes{m}", align_bytes=64) for m in range(4)]
+        q_scales = [keep.tile([P, P], U8, name=f"q_scales{m}", align_bytes=64) for m in range(4)]
+
+        for t in range(T):
+            for h in range(2):
+                nc.vector.tensor_tensor(
+                    ks[h][:, t, :],
+                    books[t][:].indirect(offsets[:, 8 * h : 8 * h + 8]),
+                    norm_sb[:, HALF * h : HALF * h + HALF],
+                    MULT,
+                )
+
+        def q_raw(m):
+            return raws[m // 2][:, :, 128 * (m % 2) : 128 * (m % 2) + 128]
+
+        def quant_q(m):
+            nc.vector.quantize_mx(
+                out=q_codes[m][:].bitcast(FP8X4), scales=q_scales[m][:],
+                in_=qb[m][:].rearrange("p c t -> p (c t)"))
+
+        for m in range(3):
+            interleaved(nc.scalar.copy, qb[m][:], q_raw(m))
+
+        for h in range(2):
+            interleaved(nc.vector.tensor_copy, kb[h][:], ks[h][:])
+        for h in range(2):
+            cols = slice(HALF * h, HALF * h + HALF)
+            nc.vector.quantize_mx(
+                out=k_codes[:, cols].bitcast(FP8X4), scales=k_scales[:, cols],
+                in_=kb[h][:].rearrange("p c t -> p (c t)"))
+        quant_q(0)
+        interleaved(nc.vector.tensor_copy, qb[3][:], q_raw(3))
+        for m in range(1, 4):
+            quant_q(m)
+
+        out_rows = out[0].rearrange("(m p) n -> m p n", p=P)
+        for m in range(4):
+            acc = psum.tile([P, N], F32, name=f"acc{m}")
+            nc.tensor.matmul_mx(
+                out=acc[:],
+                lhsT=q_codes[m][:].bitcast(FP8X4), lhsT_scale=q_scales[m][:],
+                rhs=k_codes[:].bitcast(FP8X4), rhs_scale=k_scales[:],
+                start=True, stop=True)
+            res = keep.tile([P, N], F32, name=f"res{m}")
+            if m % 2 == 0:
+                nc.scalar.copy(out=res[:], in_=acc[:])
+            else:
+                nc.vector.tensor_copy(out=res[:], in_=acc[:])
+            nc.sync.dma_start(out_rows[m], res[:])

@@ -11,19 +11,9 @@ U32 = mybir.dt.uint32
 U8 = mybir.dt.uint8
 FP8X4 = mybir.dt.float8_e4m3fn_x4
 MULT = mybir.AluOpType.mult
-
 P = 128
 T = 4
-HALF = 128
-
 FLOPS = 2 * D * Q * N
-
-
-def interleaved(nc_copy, dst, src):
-    nc_copy(
-        out=dst.rearrange("p (c i) t -> p c t i", i=4),
-        in_=src.rearrange("p t (c i) -> p c t i", i=4),
-    )
 
 
 def tile_attend_pq_lin_kernel(tc, qT, cb, norm, offs, out):
@@ -31,82 +21,135 @@ def tile_attend_pq_lin_kernel(tc, qT, cb, norm, offs, out):
     with ExitStack() as ctx:
         keep = ctx.enter_context(tc.tile_pool(name="keep", bufs=1))
         psum = ctx.enter_context(tc.psum_pool(name="psum", bufs=1))
-
         offsets = keep.tile([P, N // 16], U16, name="offsets")
-        nc.sync.dma_start(offsets[:], offs)
         norm_sb = keep.tile([P, N], F32, name="norm_sb")
-        nc.sync.dma_start(norm_sb[:], norm)
-
         cb_rows = cb.rearrange("(p t) c -> p t c", t=T)
-        books = []
-        for t in range(T):
-            book = keep.tile([P, C], F32, name=f"book{t}")
-            nc.sync.dma_start(book[:], cb_rows[:, t, :])
-            books.append(book)
-
+        books = [keep.tile([P, C], F32, name=f"book{t}") for t in range(T)]
         q_rows = qT[0].rearrange("(p t) q -> p t q", t=T)
-        raws = []
-        for h in range(2):
-            raw = keep.tile([P, T, 256], F32, name=f"raw{h}")
-            nc.sync.dma_start(raw[:], q_rows[:, :, 256 * h : 256 * h + 256])
-            raws.append(raw)
+        q_cuts = [[0,256],[256,512]]
+        raws = [keep.tile([P, T, b - a], F32, name=f"raw{a}") for a, b in q_cuts]
+
+        def ld_offs():
+            nc.sync.dma_start(offsets[:], offs)
+
+        def ld_norm():
+            nc.sync.dma_start(norm_sb[:], norm)
+
+        def ld_cb(t):
+            nc.sync.dma_start(books[t][:], cb_rows[:, t, :])
+
+        def ld_q(i):
+            a, b = q_cuts[i]
+            nc.sync.dma_start(raws[i][:], q_rows[:, :, a:b])
 
         dummy = keep.tile([P, 1], F32, name="dummy")
         dummy2 = keep.tile([P, 1], F32, name="dummy2")
         nc.gpsimd.memset(dummy[:], 0.0)
         nc.scalar.copy(out=dummy2[:], in_=dummy[:])
 
-        ks = [keep.tile([P, T, HALF], F32, name=f"ks{h}") for h in range(2)]
-        kb = [keep.tile([P, HALF, T], BF16, name=f"kb{h}", align_bytes=64) for h in range(2)]
+        ks = keep.tile([P, T, N], F32, name="ks")
+        kb = keep.tile([P, N, T], BF16, name="kb", align_bytes=64)
         k_codes = keep.tile([P, N], U32, name="k_codes", align_bytes=64)
         k_scales = keep.tile([P, N], U8, name="k_scales", align_bytes=64)
         qb = [keep.tile([P, P, T], BF16, name=f"qb{m}", align_bytes=64) for m in range(4)]
         q_codes = [keep.tile([P, P], U32, name=f"q_codes{m}", align_bytes=64) for m in range(4)]
         q_scales = [keep.tile([P, P], U8, name=f"q_scales{m}", align_bytes=64) for m in range(4)]
 
-        for t in range(T):
-            for h in range(2):
-                nc.vector.tensor_tensor(
-                    ks[h][:, t, :],
-                    books[t][:].indirect(offsets[:, 8 * h : 8 * h + 8]),
-                    norm_sb[:, HALF * h : HALF * h + HALF],
-                    MULT,
-                )
+        def weave(copy, dst, src):
+            copy(
+                out=dst.rearrange("p (c i) t -> p c t i", i=4),
+                in_=src.rearrange("p t (c i) -> p c t i", i=4),
+            )
 
-        def q_raw(m):
-            return raws[m // 2][:, :, 128 * (m % 2) : 128 * (m % 2) + 128]
+        engines = {"v": nc.vector.tensor_copy, "s": nc.scalar.copy, "g": nc.gpsimd.tensor_copy}
 
-        def quant_q(m):
+        def gather(t):
+            nc.vector.tensor_tensor(ks[:, t, :], books[t][:].indirect(offsets[:]), norm_sb[:], MULT)
+
+        def gather_half(t, h):
+            cols = slice(128 * h, 128 * h + 128)
+            nc.vector.tensor_tensor(
+                ks[:, t, cols], books[t][:].indirect(offsets[:, 8 * h : 8 * h + 8]), norm_sb[:, cols], MULT)
+
+        def ki(e, a, b):
+            weave(engines[e], kb[:, a:b, :], ks[:, :, a:b])
+
+        def kq(a, b):
+            nc.vector.quantize_mx(
+                out=k_codes[:, a:b].bitcast(FP8X4), scales=k_scales[:, a:b],
+                in_=kb[:, a:b, :].rearrange("p c t -> p (c t)"))
+
+        def qi(e, m, a, b):
+            lo = 128 * m + a
+            for i, (x, y) in enumerate(q_cuts):
+                if x <= lo < y:
+                    weave(engines[e], qb[m][:, a:b, :], raws[i][:, :, lo - x : lo - x + b - a])
+
+        def qq(m):
             nc.vector.quantize_mx(
                 out=q_codes[m][:].bitcast(FP8X4), scales=q_scales[m][:],
                 in_=qb[m][:].rearrange("p c t -> p (c t)"))
 
-        for m in range(3):
-            interleaved(nc.scalar.copy, qb[m][:], q_raw(m))
-
-        for h in range(2):
-            interleaved(nc.vector.tensor_copy, kb[h][:], ks[h][:])
-        for h in range(2):
-            cols = slice(HALF * h, HALF * h + HALF)
-            nc.vector.quantize_mx(
-                out=k_codes[:, cols].bitcast(FP8X4), scales=k_scales[:, cols],
-                in_=kb[h][:].rearrange("p c t -> p (c t)"))
-        quant_q(0)
-        interleaved(nc.vector.tensor_copy, qb[3][:], q_raw(3))
-        for m in range(1, 4):
-            quant_q(m)
-
         out_rows = out[0].rearrange("(m p) n -> m p n", p=P)
-        for m in range(4):
-            acc = psum.tile([P, N], F32, name=f"acc{m}")
+        accs = {}
+        ress = {}
+
+        def mm(m, a=0, b=N):
+            acc = psum.tile([P, b - a], F32, name=f"acc{m}_{a}")
+            accs[(m, a)] = acc
             nc.tensor.matmul_mx(
                 out=acc[:],
                 lhsT=q_codes[m][:].bitcast(FP8X4), lhsT_scale=q_scales[m][:],
-                rhs=k_codes[:].bitcast(FP8X4), rhs_scale=k_scales[:],
+                rhs=k_codes[:, a:b].bitcast(FP8X4), rhs_scale=k_scales[:, a:b],
                 start=True, stop=True)
-            res = keep.tile([P, N], F32, name=f"res{m}")
-            if m % 2 == 0:
-                nc.scalar.copy(out=res[:], in_=acc[:])
-            else:
-                nc.vector.tensor_copy(out=res[:], in_=acc[:])
-            nc.sync.dma_start(out_rows[m], res[:])
+
+        def ev(e, m, a=0, b=N):
+            if m not in ress:
+                ress[m] = keep.tile([P, N], F32, name=f"res{m}")
+            engines[e](out=ress[m][:, a:b], in_=accs[(m, a)][:])
+
+        def st(m, q="sync"):
+            (nc.sync if q == "sync" else nc.scalar).dma_start(out_rows[m], ress[m][:])
+
+        ld_offs()
+        ld_norm()
+        ld_cb(0)
+        ld_cb(1)
+        ld_cb(2)
+        ld_cb(3)
+        ld_q(0)
+        ld_q(1)
+        gather_half(0, 0)
+        gather_half(0, 1)
+        gather_half(1, 0)
+        gather_half(1, 1)
+        gather_half(2, 0)
+        gather_half(2, 1)
+        gather_half(3, 0)
+        gather_half(3, 1)
+        ki("v", 0, 128)
+        ki("v", 128, 256)
+        qi("s", 0, 0, 128)
+        qi("v", 1, 0, 128)
+        kq(0, 256)
+        qq(1)
+        qq(0)
+        mm(1)
+        mm(0)
+        ev("s", 0)
+        st(0)
+        ev("v", 1)
+        st(1)
+        qi("s", 2, 0, 96)
+        qi("v", 3, 0, 128)
+        qi("v", 2, 96, 128)
+        qq(3)
+        mm(3)
+        qq(2)
+        ev("s", 3)
+        st(3)
+        mm(2, 0, 128)
+        mm(2, 128, 256)
+        ev("v", 2, 0, 128)
+        ev("s", 2, 128, 256)
+        st(2)

@@ -119,6 +119,9 @@ def tile_attend_pq_lin_kernel(tc, qT, cb, norm, offs, out):
         ld_cb(3)
         ld_q(0)
         ld_q(1)
+        qi("s", 0, 0, 128)
+        qi("s", 1, 0, 128)
+        qi("s", 2, 0, 96)
         gather_half(0, 0)
         gather_half(0, 1)
         gather_half(1, 0)
@@ -129,27 +132,25 @@ def tile_attend_pq_lin_kernel(tc, qT, cb, norm, offs, out):
         gather_half(3, 1)
         ki("v", 0, 128)
         ki("v", 128, 256)
-        qi("s", 0, 0, 128)
-        qi("v", 1, 0, 128)
-        kq(0, 256)
-        qq(1)
+        kq(0, 128)
+        kq(128, 256)
         qq(0)
-        mm(1)
         mm(0)
-        ev("s", 0)
-        st(0)
-        ev("v", 1)
-        st(1)
-        qi("s", 2, 0, 96)
         qi("v", 3, 0, 128)
+        qq(1)
+        mm(1)
         qi("v", 2, 96, 128)
         qq(3)
         mm(3)
         qq(2)
-        ev("s", 3)
-        st(3)
         mm(2, 0, 128)
         mm(2, 128, 256)
+        ev("s", 0)
+        st(0)
+        ev("v", 1)
+        st(1)
+        ev("s", 3)
+        st(3)
         ev("v", 2, 0, 128)
         ev("s", 2, 128, 256)
         st(2)

@@ -22,7 +22,7 @@ def tile_attend_pq_lin_kernel(tc, qT, cb, norm, offs, out):
         keep = ctx.enter_context(tc.tile_pool(name="keep", bufs=1))
         psum = ctx.enter_context(tc.psum_pool(name="psum", bufs=1))
         offsets = keep.tile([P, N // 16], U16, name="offsets")
-        norm_sb = keep.tile([P, N], F32, name="norm_sb")
+        norm_h = [keep.tile([P, 128], F32, name=f"norm{h}") for h in range(2)]
         cb_rows = cb.rearrange("(p t) c -> p t c", t=T)
         books = [keep.tile([P, C], F32, name=f"book{t}") for t in range(T)]
         q_rows = qT[0].rearrange("(p t) q -> p t q", t=T)
@@ -32,8 +32,8 @@ def tile_attend_pq_lin_kernel(tc, qT, cb, norm, offs, out):
         def ld_offs():
             nc.sync.dma_start(offsets[:], offs)
 
-        def ld_norm():
-            nc.sync.dma_start(norm_sb[:], norm)
+        def ld_norm(h):
+            nc.sync.dma_start(norm_h[h][:], norm[:, 128 * h : 128 * h + 128])
 
         def ld_cb(t):
             nc.sync.dma_start(books[t][:], cb_rows[:, t, :])
@@ -63,13 +63,10 @@ def tile_attend_pq_lin_kernel(tc, qT, cb, norm, offs, out):
 
         engines = {"v": nc.vector.tensor_copy, "s": nc.scalar.copy, "g": nc.gpsimd.tensor_copy}
 
-        def gather(t):
-            nc.vector.tensor_tensor(ks[:, t, :], books[t][:].indirect(offsets[:]), norm_sb[:], MULT)
-
         def gather_half(t, h):
             cols = slice(128 * h, 128 * h + 128)
             nc.vector.tensor_tensor(
-                ks[:, t, cols], books[t][:].indirect(offsets[:, 8 * h : 8 * h + 8]), norm_sb[:, cols], MULT)
+                ks[:, t, cols], books[t][:].indirect(offsets[:, 8 * h : 8 * h + 8]), norm_h[h][:], MULT)
 
         def ki(e, a, b):
             weave(engines[e], kb[:, a:b, :], ks[:, :, a:b])
@@ -112,8 +109,9 @@ def tile_attend_pq_lin_kernel(tc, qT, cb, norm, offs, out):
             (nc.sync if q == "sync" else nc.scalar).dma_start(out_rows[m], ress[m][:])
 
         ld_offs()
-        ld_norm()
+        ld_norm(0)
         ld_cb(0)
+        ld_norm(1)
         ld_cb(1)
         ld_cb(2)
         ld_cb(3)
@@ -152,5 +150,5 @@ def tile_attend_pq_lin_kernel(tc, qT, cb, norm, offs, out):
         ev("s", 3)
         st(3)
         ev("v", 2, 0, 128)
-        ev("s", 2, 128, 256)
+        ev("v", 2, 128, 256)
         st(2)

from contextlib import ExitStack

import concourse.mybir as mybir

D, C, N, Q = 512, 512, 256, 512

F32 = mybir.dt.float32
BF16 = mybir.dt.bfloat16
U16 = mybir.dt.uint16
U32 = mybir.dt.uint32
U8 = mybir.dt.uint8
FP8X4 = mybir.dt.float8_e4m3fn_x4
MULT = mybir.AluOpType.mult
P = 128
T = 4
FLOPS = 2 * D * Q * N


def tile_attend_pq_lin_kernel(tc, qT, cb, norm, offs, out):
    nc = tc.nc
    with ExitStack() as ctx:
        keep = ctx.enter_context(tc.tile_pool(name="keep", bufs=1))
        psum = ctx.enter_context(tc.psum_pool(name="psum", bufs=1))
        offsets = keep.tile([P, N // 16], U16, name="offsets")
        norm_h = [keep.tile([P, 128], F32, name=f"norm{h}") for h in range(2)]
        cb_rows = cb.rearrange("(p t) c -> p t c", t=T)
        books = [keep.tile([P, C], F32, name=f"book{t}") for t in range(T)]
        q_rows = qT[0].rearrange("(p t) q -> p t q", t=T)
        q_cuts = [[0,256],[256,512]]
        raws = [keep.tile([P, T, b - a], F32, name=f"raw{a}") for a, b in q_cuts]

        def ld_offs():
            nc.sync.dma_start(offsets[:], offs)

        def ld_norm(h):
            nc.sync.dma_start(norm_h[h][:], norm[:, 128 * h : 128 * h + 128])

        def ld_cb(t):
            nc.sync.dma_start(books[t][:], cb_rows[:, t, :])

        def ld_q(i):
            a, b = q_cuts[i]
            nc.sync.dma_start(raws[i][:], q_rows[:, :, a:b])

        dummy = keep.tile([P, 1], F32, name="dummy")
        dummy2 = keep.tile([P, 1], F32, name="dummy2")
        nc.gpsimd.memset(dummy[:], 0.0)
        nc.scalar.copy(out=dummy2[:], in_=dummy[:])

        ks = keep.tile([P, T, N], F32, name="ks")
        kb = keep.tile([P, N, T], BF16, name="kb", align_bytes=64)
        k_codes = keep.tile([P, N], U32, name="k_codes", align_bytes=64)
        k_scales = keep.tile([P, N], U8, name="k_scales", align_bytes=64)
        qb = [keep.tile([P, P, T], BF16, name=f"qb{m}", align_bytes=64) for m in range(4)]
        q_codes = [keep.tile([P, P], U32, name=f"q_codes{m}", align_bytes=64) for m in range(4)]
        q_scales = [keep.tile([P, P], U8, name=f"q_scales{m}", align_bytes=64) for m in range(4)]

        def weave(copy, dst, src):
            copy(
                out=dst.rearrange("p (c i) t -> p c t i", i=4),
                in_=src.rearrange("p t (c i) -> p c t i", i=4),
            )

        engines = {"v": nc.vector.tensor_copy, "s": nc.scalar.copy, "g": nc.gpsimd.tensor_copy}

        def gather_half(t, h):
            cols = slice(128 * h, 128 * h + 128)
            nc.vector.tensor_tensor(
                ks[:, t, cols], books[t][:].indirect(offsets[:, 8 * h : 8 * h + 8]), norm_h[h][:], MULT)

        def ki(e, a, b):
            weave(engines[e], kb[:, a:b, :], ks[:, :, a:b])

        def kq(a, b):
            nc.vector.quantize_mx(
                out=k_codes[:, a:b].bitcast(FP8X4), scales=k_scales[:, a:b],
                in_=kb[:, a:b, :].rearrange("p c t -> p (c t)"))

        def qi(e, m, a, b):
            lo = 128 * m + a
            for i, (x, y) in enumerate(q_cuts):
                if x <= lo < y:
                    weave(engines[e], qb[m][:, a:b, :], raws[i][:, :, lo - x : lo - x + b - a])

        def qq(m):
            nc.vector.quantize_mx(
                out=q_codes[m][:].bitcast(FP8X4), scales=q_scales[m][:],
                in_=qb[m][:].rearrange("p c t -> p (c t)"))

        out_rows = out[0].rearrange("(m p) n -> m p n", p=P)
        accs = {}
        ress = {}

        def mm(m, a=0, b=N):
            acc = psum.tile([P, b - a], F32, name=f"acc{m}_{a}")
            accs[(m, a)] = acc
            nc.tensor.matmul_mx(
                out=acc[:],
                lhsT=q_codes[m][:].bitcast(FP8X4), lhsT_scale=q_scales[m][:],
                rhs=k_codes[:, a:b].bitcast(FP8X4), rhs_scale=k_scales[:, a:b],
                start=True, stop=True)

        def ev(e, m, a=0, b=N):
            if m not in ress:
                ress[m] = keep.tile([P, N], F32, name=f"res{m}")
            engines[e](out=ress[m][:, a:b], in_=accs[(m, a)][:])

        def st(m, q="sync"):
            (nc.sync if q == "sync" else nc.scalar).dma_start(out_rows[m], ress[m][:])

        ld_offs()
        ld_norm(0)
        ld_cb(0)
        ld_norm(1)
        ld_cb(1)
        ld_cb(2)
        ld_cb(3)
        ld_q(0)
        ld_q(1)
        qi("s", 0, 0, 128)
        qi("s", 1, 0, 128)
        qi("s", 2, 0, 96)
        gather_half(0, 0)
        gather_half(0, 1)
        gather_half(1, 0)
        gather_half(1, 1)
        gather_half(2, 0)
        gather_half(2, 1)
        gather_half(3, 0)
        gather_half(3, 1)
        ki("v", 0, 128)
        ki("v", 128, 256)
        kq(0, 128)
        kq(128, 256)
        qq(0)
        mm(0)
        qi("v", 3, 0, 128)
        qq(1)
        mm(1)
        qi("v", 2, 96, 128)
        qq(3)
        mm(3)
        qq(2)
        mm(2, 0, 128)
        mm(2, 128, 256)
        ev("s", 0)
        st(0)
        ev("v", 1)
        st(1)
        ev("s", 3)
        st(3)
        ev("v", 2, 0, 128)
        ev("v", 2, 128, 256)
        st(2)
